import numpy as np
import ml_dtypes


def mxq(x, axis, fmt="e4m3"):
    dtype, down = {"e4m3": (ml_dtypes.float8_e4m3fn, 7), "e5m2": (ml_dtypes.float8_e5m2, 14)}[fmt]
    v = np.moveaxis(np.asarray(x, np.float32).astype(ml_dtypes.bfloat16).astype(np.float64), axis, -1)
    blocks = v.reshape(v.shape[:-1] + (-1, 32))
    amax = np.abs(blocks).max(-1, keepdims=True)
    byte = np.maximum(np.where(amax > 0, np.frexp(amax)[1] - 1 + 127, 0) - down, 1)
    scale = np.exp2(byte - 127.0)
    codes = (blocks / scale).astype(np.float32).astype(dtype).astype(np.float64)
    return np.moveaxis((codes * scale).reshape(v.shape), -1, axis)


WIDE = False


def mx_kscale(k):
    if not WIDE:
        return np.ones(k)
    levels = np.array([10, -10, 5, -5, 0])
    if k % 512:
        return np.exp2(np.random.permutation(np.resize(levels, k // 32))).repeat(32)
    a = np.empty((k // 512, 16))
    for p in range(k // 512):
        a[p, :8] = np.random.permutation(np.resize(levels, 8))
        for g in range(8):
            far = levels[np.abs(levels - a[p, g]) >= 10]
            a[p, g + 8] = far[np.random.randint(len(far))]
    return np.exp2(a.ravel()).repeat(32)


def f64(x):
    return np.asarray(x).astype(np.float64)


def striped(idx):
    return np.tile(idx.reshape(-1, 16).T, (8, 1)).astype(np.uint16)


def unstriped(offs):
    return offs[:16].T.reshape(-1).astype(np.int64)


def pack_weight(w):
    k, n = w.shape
    w = f64(np.asarray(w, np.float32).astype(ml_dtypes.bfloat16)).reshape(k // 32, 32, n)
    amax = np.abs(w).max(1)
    byte = np.clip(np.where(amax > 0, np.frexp(amax)[1] - 1 + 127 - 7, 1), 1, 254)
    scaled = (w * np.exp2(127.0 - byte)[:, None, :]).reshape(k, n).astype(np.float32)
    words = np.ascontiguousarray(scaled.reshape(k // 512, 128, 4, n).transpose(0, 1, 3, 2)).astype(ml_dtypes.float8_e4m3fn).view(np.uint8)
    return words, np.ascontiguousarray(byte.astype(np.uint8).reshape(k // 512, 16, n))


def unpack_weight(words, scales):
    g, p, n, _ = words.shape
    vals = np.ascontiguousarray(words).view(ml_dtypes.float8_e4m3fn).astype(np.float64) * np.repeat(np.exp2(scales.astype(np.float64) - 127.0), 8, axis=1)[..., None]
    return vals.transpose(0, 1, 3, 2).reshape(g * 512, n)


E2M1 = np.array([0.0, 0.5, 1.0, 1.5, 2.0, 3.0, 4.0, 6.0, -0.0, -0.5, -1.0, -1.5, -2.0, -3.0, -4.0, -6.0])


def pack_fp4(w):
    k, n = w.shape
    w = f64(np.asarray(w, np.float32).astype(ml_dtypes.bfloat16)).reshape(k // 32, 32, n)
    amax = np.abs(w).max(1)
    mant, ex = np.frexp(amax / 6.0)
    byte = np.clip(np.where(amax > 0, np.where(mant > 0.5, ex, ex - 1) + 127, 1), 1, 254)
    scaled = (w * np.exp2(127.0 - byte)[:, None, :]).reshape(k, n).astype(np.float32)
    c = np.ascontiguousarray(scaled.reshape(k // 512, 128, 4, n).transpose(0, 1, 3, 2)).astype(ml_dtypes.float4_e2m1fn).view(np.uint8) & 0xF
    words = (c[..., 0::2] | (c[..., 1::2] << 4)).reshape(k // 512, 128, 2 * n)
    return np.ascontiguousarray(words), np.ascontiguousarray(byte.astype(np.uint8).reshape(k // 512, 16, n))


def unpack_fp4(words, scales):
    g, _, n = scales.shape
    words = np.ascontiguousarray(words).reshape(g, 128, n, 2)
    nib = np.empty((g, 128, n, 4), np.uint8)
    nib[..., 0::2] = words & 0xF
    nib[..., 1::2] = words >> 4
    vals = E2M1[nib] * np.repeat(np.exp2(scales.astype(np.float64) - 127.0), 8, axis=1)[..., None]
    return vals.transpose(0, 1, 3, 2).reshape(g * 512, n)


def relu(v):
    return np.maximum(v, 0.0)


K, T, S, D, N, H, V, U = 512, 2048, 1024, 4, 128, 512, 256, 512


def setup_inputs():
    n = np.random.standard_normal
    s = mx_kscale(K)[:, None]
    u = mx_kscale(H)
    packed_xT = pack_weight(n((K, T)) * s)
    packed_w1 = pack_fp4(n((K, H)) / np.sqrt(K) / s)
    packed_w2 = pack_fp4(n((K, H)) / np.sqrt(K) / s)
    packed_w3 = pack_fp4(n((H, N)) / np.sqrt(H) / u[:, None])
    return {
        "x_words": packed_xT[0],
        "x_scales": packed_xT[1],
        "w1_words": packed_w1[0],
        "w1_scales": packed_w1[1],
        "w2_words": packed_w2[0],
        "w2_scales": packed_w2[1],
        "dz": (np.random.uniform(0.3, 1.2, (H, S))).astype(np.float32),
        "unit": (np.random.uniform(0.6, 1.4, (H, 1)) * u[:, None]).astype(np.float32),
        "w3_words": packed_w3[0],
        "w3_scales": packed_w3[1],
        "offs": striped(np.random.permutation(T)[:S]),
        "env": striped(np.random.permutation(S)),
        "stn": striped(np.random.permutation(np.concatenate([np.arange(V), np.random.randint(0, V, U - V)]))),
    }


def reference(x_words, x_scales, w1_words, w1_scales, w2_words, w2_scales, dz, unit, w3_words, w3_scales, offs, env, stn):
    xq = unpack_weight(x_words, x_scales)[:, unstriped(offs)]
    tp = unpack_fp4(w1_words, w1_scales).T @ xq
    temp = np.tanh(tp)
    wv = unpack_fp4(w2_words, w2_scales).T @ xq
    moist = np.log(np.exp(wv) + 1.0)
    thetae = (temp + 1.5) * (np.exp(0.6 * np.tanh(moist)))
    te = thetae[:, unstriped(env)]
    buoy = thetae - te
    cl_ = relu(buoy) * f64(dz)
    cape = cl_.reshape(len(cl_), -1, D).sum(axis=2)
    cs = cape[:, unstriped(stn)]
    nb_ = relu(-1.0 * buoy)
    cin = nb_.reshape(len(nb_), -1, D).max(axis=2)
    is_ = cin[:, unstriped(stn)]
    hid = f64(unit) * (cs * np.exp(-1.0 * is_))
    return unpack_fp4(w3_words, w3_scales).T @ mxq(hid, 0, "e4m3")

@@ -1,0 +1,163 @@
+from contextlib import ExitStack
+
+import concourse.mybir as mybir
+
+K, T, S, D, N, H, V, U = 512, 2048, 1024, 4, 128, 512, 256, 512
+FLOPS = 2 * (2 * K * H * S) + 2 * H * N * U
+
+F32 = mybir.dt.float32
+BF16 = mybir.dt.bfloat16
+I32 = mybir.dt.int32
+U32 = mybir.dt.uint32
+U16 = mybir.dt.uint16
+U8 = mybir.dt.uint8
+FP8X4 = mybir.dt.float8_e4m3fn_x4
+FP4X4 = mybir.dt.float4_e2m1fn_x4
+ACT = mybir.ActivationFunctionType
+ALU = mybir.AluOpType
+
+P = 128
+PACK = 4
+BANK = 512
+LN_FLOOR = 2.0 ** -60
+
+
+def tile_picked_yweathr_exp_p_kernel(tc, x_words, x_scales, w1_words, w1_scales, w2_words, w2_scales, dz, unit, w3_words, w3_scales, offs, env, stn, out):
+    nc = tc.nc
+    with ExitStack() as ctx:
+        keep = ctx.enter_context(tc.tile_pool(name="keep", bufs=1))
+        psum = ctx.enter_context(tc.psum_pool(name="psum", bufs=8))
+
+        def sbuf(name, width, dtype, tag=None):
+            return keep.tile([P, width], dtype, name=name, tag=tag or name, align_bytes=64)
+
+        def load_scale_rows(queue, plane, scales):
+            for q in range(4):
+                queue.dma_start(out=plane[32 * q : 32 * q + 4, :].bitcast(I32), in_=scales[0, 4 * q : 4 * q + 4, :].bitcast(I32))
+
+        offs_t = keep.tile([P, S // 16], U16, name="offs_t")
+        env_t = keep.tile([P, S // 16], U16, name="env_t")
+        stn_t = keep.tile([P, U // 16], U16, name="stn_t")
+
+        xw = sbuf("xw", T, U32)
+        xs = sbuf("xs", T, U8)
+        w2w, w2s = sbuf("w2w", 2 * H, U8, "raw_words"), sbuf("w2s", H, U8, "raw_scales")
+        nc.vector.memset(xs[:].bitcast(I32), 0)
+        nc.gpsimd.memset(w2s[:].bitcast(I32), 0)
+
+        nc.sync.dma_start(offs_t[:], offs)
+        nc.sync.dma_start(out=w2w[:].bitcast(I32), in_=w2_words[0].bitcast(I32))
+        nc.sync.dma_start(out=xw[:].bitcast(I32), in_=x_words[0].rearrange("p n t -> p (n t)").bitcast(I32))
+        load_scale_rows(nc.scalar, xs, x_scales)
+        load_scale_rows(nc.gpsimd, w2s, w2_scales)
+        nc.sync.dma_start(env_t[:], env)
+        nc.sync.dma_start(stn_t[:], stn)
+
+        def deal(name, words, scales):
+            dw, ds = sbuf(name + "_dw", 2 * H, U8), sbuf(name + "_ds", H, U8)
+            nc.vector.tensor_copy(out=dw[:].rearrange("p (t m b) -> p t m b", t=PACK, b=2), in_=words[:].rearrange("p (m t b) -> p t m b", t=PACK, b=2))
+            nc.vector.tensor_copy(out=ds[:].rearrange("p (t m) -> p t m", t=PACK), in_=scales[:].rearrange("p (m t) -> p t m", t=PACK))
+            return dw, ds
+
+        halves = [slice(h * BANK, (h + 1) * BANK) for h in range(S // BANK)]
+        list_halves = [slice(h * BANK // 16, (h + 1) * BANK // 16) for h in range(S // BANK)]
+        xgw = [sbuf(f"xgw{h}", BANK, U32) for h in range(2)]
+        xgs = [sbuf(f"xgs{h}", BANK, U8) for h in range(2)]
+
+        w2d = deal("w2", w2w, w2s)
+        for h in range(2):
+            nc.vector.tensor_copy(out=xgs[h][:], in_=xs[:].indirect(offs_t[:, list_halves[h]]))
+            nc.vector.tensor_copy(out=xgw[h][:], in_=xw[:].indirect(offs_t[:, list_halves[h]]))
+        w1w, w1s = sbuf("w1w", 2 * H, U8, "raw_words"), sbuf("w1s", H, U8, "raw_scales")
+        nc.gpsimd.memset(w1s[:].bitcast(I32), 0)
+        nc.sync.dma_start(out=w1w[:].bitcast(I32), in_=w1_words[0].bitcast(I32))
+        load_scale_rows(nc.sync, w1s, w1_scales)
+        w1d = deal("w1", w1w, w1s)
+        w3w, w3s = sbuf("w3w", 2 * N, U8, "raw_words"), sbuf("w3s", N, U8, "raw_scales")
+        nc.gpsimd.memset(w3s[:].bitcast(I32), 0)
+        nc.sync.dma_start(out=w3w[:].bitcast(I32), in_=w3_words[0].bitcast(I32))
+        load_scale_rows(nc.sync, w3s, w3_scales)
+        dz_t = keep.tile([P, PACK, S], F32, name="dz_t", tag="xw", align_bytes=64)
+        nc.sync.dma_start(out=dz_t[:], in_=dz.rearrange("(p t) j -> p t j", t=PACK))
+        unit_t = sbuf("unit_t", PACK, F32, "xs")
+        nc.sync.dma_start(out=unit_t[:], in_=unit.rearrange("(p t) o -> p (t o)", t=PACK))
+
+        def product(wd, t, h):
+            acc = psum.tile([P, BANK], F32, name="bank")
+            nc.tensor.matmul_mx(out=acc[:], lhsT=wd[0][:, 2 * P * t : 2 * P * (t + 1)].bitcast(FP4X4), lhsT_scale=wd[1][:, P * t : P * (t + 1)],
+                                rhs=xgw[h][:].bitcast(FP8X4), rhs_scale=xgs[h][:], start=True, stop=True)
+            return acc
+
+        moist = sbuf("moist", PACK * S, F32)
+        for h in range(2):
+            for t in range(PACK):
+                wv = product(w2d, t, h)
+                nc.scalar.activation(out=moist[:, t * S + h * BANK : t * S + (h + 1) * BANK], in_=wv[:], func=ACT.Sigmoid, scale=-1.0)
+        nc.scalar.activation(out=moist[:], in_=moist[:], func=ACT.Ln, bias=LN_FLOOR)
+
+        planes = keep.tile([P, PACK, U], BF16, name="planes", align_bytes=64)
+        theta = [sbuf(f"theta{t}", S, F32) for t in range(PACK)]
+        other = [sbuf(f"other{t}", S, F32) for t in range(PACK)]
+        sink = [sbuf(f"sink{t}", S, F32) for t in range(PACK)]
+
+        def make_theta(t):
+            temp = sbuf(f"temp{t}", S, F32)
+            for h in range(2):
+                tp = product(w1d, t, h)
+                nc.scalar.activation(out=temp[:, halves[h]], in_=tp[:], func=ACT.Tanh)
+            gain = moist[:, t * S : (t + 1) * S]
+            nc.scalar.activation(out=gain, in_=gain, func=ACT.Tanh, scale=-1.0)
+            nc.scalar.activation(out=gain, in_=gain, func=ACT.Exp, scale=0.6)
+            nc.vector.scalar_tensor_tensor(out=theta[t][:], in0=temp[:], scalar=1.5, in1=gain, op0=ALU.add, op1=ALU.mult)
+            if t == 0:
+                nc.vector.tensor_copy(out=other[t][:], in_=theta[t][:])
+            if t == 1:
+                nc.sync.dma_start(out=other[t][:], in_=theta[t][:])
+
+        def compare(t):
+            if t < 2:
+                for h in range(2):
+                    nc.vector.tensor_tensor(out=sink[t][:, halves[h]], in0=theta[t][:].indirect(env_t[:, list_halves[h]]), in1=other[t][:, halves[h]], op=ALU.subtract)
+            else:
+                for h in range(2):
+                    nc.scalar.activation(out=other[t][:, halves[h]], in_=theta[t][:].indirect(env_t[:, list_halves[h]]), func=ACT.Copy)
+                nc.vector.tensor_tensor(out=sink[t][:], in0=other[t][:], in1=theta[t][:], op=ALU.subtract)
+
+        def integrate(t):
+            table = sbuf(f"table{t}", 4 * V, F32)
+            hid_v, cin, pair = table[:, 0:V], table[:, V : 2 * V], table[:, 2 * V : 4 * V]
+            pair2 = pair.rearrange("p (v e) -> p v e", e=2)
+            sink4 = sink[t][:].rearrange("p (v a e) -> p v a e", a=2, e=2)
+            nc.vector.tensor_tensor(out=pair2, in0=sink4[:, :, 0, :], in1=sink4[:, :, 1, :], op=ALU.max)
+            lift = sbuf(f"lift{t}", S, F32)
+            nc.vector.scalar_tensor_tensor(out=lift[:], in0=sink[t][:], scalar=0.0, in1=dz_t[:, t, :], op0=ALU.min, op1=ALU.mult)
+            nc.vector.scalar_tensor_tensor(out=cin, in0=pair2[:, :, 0], scalar=0.0, in1=pair2[:, :, 1], op0=ALU.max, op1=ALU.max)
+            nc.scalar.activation(out=cin, in_=cin, func=ACT.Exp, scale=-1.0)
+            lift4 = lift[:].rearrange("p (v a e) -> p v a e", a=2, e=2)
+            sums = sbuf(f"sums{t}", 2 * V, F32)
+            sums2 = sums[:].rearrange("p (v e) -> p v e", e=2)
+            nc.vector.tensor_tensor(out=sums2, in0=lift4[:, :, 0, :], in1=lift4[:, :, 1, :], op=ALU.add)
+            cape = sbuf(f"cape{t}", V, F32)
+            nc.vector.scalar_tensor_tensor(out=cape[:], in0=sums2[:, :, 0], scalar=-1.0, in1=sums2[:, :, 1], op0=ALU.mult, op1=ALU.subtract)
+            nc.vector.scalar_tensor_tensor(out=hid_v, in0=cape[:], scalar=unit_t[:, t : t + 1], in1=cin, op0=ALU.mult, op1=ALU.mult)
+            nc.scalar.activation(out=planes[:, t, :], in_=table[:].indirect(stn_t[:]), func=ACT.Copy)
+
+        make_theta(0)
+        for t in range(PACK):
+            compare(t)
+            if t + 1 < PACK:
+                make_theta(t + 1)
+            integrate(t)
+
+        half = U // 2
+        for h in range(2):
+            cols = slice(h * half, (h + 1) * half)
+            woven = keep.tile([P, half, PACK], BF16, name=f"woven{h}", align_bytes=64)
+            nc.vector.tensor_copy(out=woven[:].rearrange("p (c i) t -> p c t i", i=4), in_=planes[:, :, cols].rearrange("p t (c i) -> p c t i", i=4))
+            codes, scales = sbuf(f"codes{h}", half, U32), sbuf(f"scales{h}", half, U8)
+            nc.vector.quantize_mx(out=codes[:].bitcast(FP8X4), scales=scales[:], in_=woven[:].rearrange("p c t -> p (c t)"))
+            acc = psum.tile([P, BANK], F32, name="bank")
+            nc.tensor.matmul_mx(out=acc[:, 0:half], lhsT=w3w[:].bitcast(FP4X4), lhsT_scale=w3s[:], rhs=codes[:].bitcast(FP8X4), rhs_scale=scales[:], start=True, stop=True)
+            res = sbuf(f"res{h}", half, F32)
+            nc.scalar.copy(out=res[:], in_=acc[:, 0:half])
+            nc.sync.dma_start(out=out[:, cols], in_=res[:])

@@ -1,6 +1,7 @@
 from contextlib import ExitStack
 
 import concourse.mybir as mybir
+from concourse.masks import make_identity
 
 K, T, S, D, N, H, V, U = 512, 2048, 1024, 4, 128, 512, 256, 512
 FLOPS = 2 * (2 * K * H * S) + 2 * H * N * U
@@ -20,6 +21,7 @@ P = 128
 PACK = 4
 BANK = 512
 LN_FLOOR = 2.0 ** -60
+QUARTER = S // 4
 
 
 def tile_picked_yweathr_exp_p_kernel(tc, x_words, x_scales, w1_words, w1_scales, w2_words, w2_scales, dz, unit, w3_words, w3_scales, offs, env, stn, out):
@@ -31,9 +33,9 @@ def tile_picked_yweathr_exp_p_kernel(tc, x_words, x_scales, w1_words, w1_scales,
         def sbuf(name, width, dtype, tag=None):
             return keep.tile([P, width], dtype, name=name, tag=tag or name, align_bytes=64)
 
-        def load_scale_rows(queue, plane, scales):
+        def load_scale_rows(queues, plane, scales):
             for q in range(4):
-                queue.dma_start(out=plane[32 * q : 32 * q + 4, :].bitcast(I32), in_=scales[0, 4 * q : 4 * q + 4, :].bitcast(I32))
+                queues[q].dma_start(out=plane[32 * q : 32 * q + 4, :].bitcast(I32), in_=scales[0, 4 * q : 4 * q + 4, :].bitcast(I32))
 
         offs_t = keep.tile([P, S // 16], U16, name="offs_t")
         env_t = keep.tile([P, S // 16], U16, name="env_t")
@@ -47,110 +49,165 @@ def tile_picked_yweathr_exp_p_kernel(tc, x_words, x_scales, w1_words, w1_scales,
 
         nc.sync.dma_start(offs_t[:], offs)
         nc.sync.dma_start(out=w2w[:].bitcast(I32), in_=w2_words[0].bitcast(I32))
-        nc.sync.dma_start(out=xw[:].bitcast(I32), in_=x_words[0].rearrange("p n t -> p (n t)").bitcast(I32))
-        load_scale_rows(nc.scalar, xs, x_scales)
-        load_scale_rows(nc.gpsimd, w2s, w2_scales)
         nc.sync.dma_start(env_t[:], env)
+        nc.sync.dma_start(out=xw[:].bitcast(I32), in_=x_words[0].rearrange("p n t -> p (n t)").bitcast(I32))
+        load_scale_rows([nc.scalar] * 4, xs, x_scales)
+        load_scale_rows([nc.scalar, nc.scalar, nc.gpsimd, nc.gpsimd], w2s, w2_scales)
         nc.sync.dma_start(stn_t[:], stn)
 
-        def deal(name, words, scales):
-            dw, ds = sbuf(name + "_dw", 2 * H, U8), sbuf(name + "_ds", H, U8)
-            nc.vector.tensor_copy(out=dw[:].rearrange("p (t m b) -> p t m b", t=PACK, b=2), in_=words[:].rearrange("p (m t b) -> p t m b", t=PACK, b=2))
-            nc.vector.tensor_copy(out=ds[:].rearrange("p (t m) -> p t m", t=PACK), in_=scales[:].rearrange("p (m t) -> p t m", t=PACK))
-            return dw, ds
+        def deal_words(engine, name, words):
+            dealt = sbuf(name, 2 * H, U8)
+            engine.tensor_copy(out=dealt[:].rearrange("p (t m b) -> p t m b", t=PACK, b=2), in_=words[:].rearrange("p (m t b) -> p t m b", t=PACK, b=2))
+            return dealt
+
+        def deal_scales(engine, name, scales):
+            dealt = sbuf(name, H, U8)
+            engine.tensor_copy(out=dealt[:].rearrange("p (t m) -> p t m", t=PACK), in_=scales[:].rearrange("p (m t) -> p t m", t=PACK))
+            return dealt
 
         halves = [slice(h * BANK, (h + 1) * BANK) for h in range(S // BANK)]
         list_halves = [slice(h * BANK // 16, (h + 1) * BANK // 16) for h in range(S // BANK)]
-        xgw = [sbuf(f"xgw{h}", BANK, U32) for h in range(2)]
-        xgs = [sbuf(f"xgs{h}", BANK, U8) for h in range(2)]
+        xgw, xgs = sbuf("xgw", S, U32), sbuf("xgs", S, U8)
 
-        w2d = deal("w2", w2w, w2s)
-        for h in range(2):
-            nc.vector.tensor_copy(out=xgs[h][:], in_=xs[:].indirect(offs_t[:, list_halves[h]]))
-            nc.vector.tensor_copy(out=xgw[h][:], in_=xw[:].indirect(offs_t[:, list_halves[h]]))
+        def pick(dst, src, q):
+            nc.vector.tensor_copy(out=dst[:, q * QUARTER : (q + 1) * QUARTER], in_=src[:].indirect(offs_t[:, q * QUARTER // 16 : (q + 1) * QUARTER // 16]))
+
+        w2_dw = deal_words(nc.vector, "w2_dw", w2w)
+        pick(xgs, xs, 0)
+        pick(xgw, xw, 0)
+        w2d = (w2_dw, deal_scales(nc.vector, "w2_ds", w2s))
+        for q in range(1, 4):
+            pick(xgs, xs, q)
+            pick(xgw, xw, q)
         w1w, w1s = sbuf("w1w", 2 * H, U8, "raw_words"), sbuf("w1s", H, U8, "raw_scales")
         nc.gpsimd.memset(w1s[:].bitcast(I32), 0)
         nc.sync.dma_start(out=w1w[:].bitcast(I32), in_=w1_words[0].bitcast(I32))
-        load_scale_rows(nc.sync, w1s, w1_scales)
-        w1d = deal("w1", w1w, w1s)
+        load_scale_rows([nc.sync] * 4, w1s, w1_scales)
+        w1d = (deal_words(nc.gpsimd, "w1_dw", w1w), deal_scales(nc.gpsimd, "w1_ds", w1s))
         w3w, w3s = sbuf("w3w", 2 * N, U8, "raw_words"), sbuf("w3s", N, U8, "raw_scales")
         nc.gpsimd.memset(w3s[:].bitcast(I32), 0)
         nc.sync.dma_start(out=w3w[:].bitcast(I32), in_=w3_words[0].bitcast(I32))
-        load_scale_rows(nc.sync, w3s, w3_scales)
+        load_scale_rows([nc.sync] * 4, w3s, w3_scales)
         dz_t = keep.tile([P, PACK, S], F32, name="dz_t", tag="xw", align_bytes=64)
         nc.sync.dma_start(out=dz_t[:], in_=dz.rearrange("(p t) j -> p t j", t=PACK))
         unit_t = sbuf("unit_t", PACK, F32, "xs")
         nc.sync.dma_start(out=unit_t[:], in_=unit.rearrange("(p t) o -> p (t o)", t=PACK))
 
-        def product(wd, t, h):
-            acc = psum.tile([P, BANK], F32, name="bank")
-            nc.tensor.matmul_mx(out=acc[:], lhsT=wd[0][:, 2 * P * t : 2 * P * (t + 1)].bitcast(FP4X4), lhsT_scale=wd[1][:, P * t : P * (t + 1)],
-                                rhs=xgw[h][:].bitcast(FP8X4), rhs_scale=xgs[h][:], start=True, stop=True)
-            return acc
+        def product(acc, wd, t, cols):
+            nc.tensor.matmul_mx(out=acc, lhsT=wd[0][:, 2 * P * t : 2 * P * (t + 1)].bitcast(FP4X4), lhsT_scale=wd[1][:, P * t : P * (t + 1)],
+                                rhs=xgw[:, cols].bitcast(FP8X4), rhs_scale=xgs[:, cols], start=True, stop=True)
 
         moist = sbuf("moist", PACK * S, F32)
+        moist3 = moist[:].rearrange("p (t j) -> p t j", t=PACK)
+        for q in range(4):
+            cols = slice(q * QUARTER, (q + 1) * QUARTER)
+            for u in range(2):
+                wv = psum.tile([P, 2, QUARTER], F32, name="bank")
+                for e in range(2):
+                    product(wv[:, e, :], w2d, 2 * u + e, cols)
+                nc.scalar.activation(out=moist3[:, 2 * u : 2 * u + 2, cols], in_=wv[:], func=ACT.Sigmoid, scale=-1.0)
+        ratio = sbuf("ratio", S, F32)
         for h in range(2):
-            for t in range(PACK):
-                wv = product(w2d, t, h)
-                nc.scalar.activation(out=moist[:, t * S + h * BANK : t * S + (h + 1) * BANK], in_=wv[:], func=ACT.Sigmoid, scale=-1.0)
-        nc.scalar.activation(out=moist[:], in_=moist[:], func=ACT.Ln, bias=LN_FLOOR)
+            nc.vector.tensor_tensor(out=ratio[:, halves[h]], in0=moist[:, halves[h]], in1=moist[:, halves[h]], op=ALU.mult)
+        for h in range(2):
+            nc.vector.tensor_scalar_add(out=ratio[:, halves[h]], in0=ratio[:, halves[h]], scalar1=1.0)
+        nc.vector.reciprocal(out=ratio[:], in_=ratio[:])
+        nc.scalar.activation(out=moist[:, S:], in_=moist[:, S:], func=ACT.Ln, bias=LN_FLOOR)
+
+        ident = sbuf("ident", P, F32)
+        make_identity(nc, ident[:])
 
         planes = keep.tile([P, PACK, U], BF16, name="planes", align_bytes=64)
+        temp = [sbuf(f"temp{t}", S, F32) for t in range(PACK)]
         theta = [sbuf(f"theta{t}", S, F32) for t in range(PACK)]
         other = [sbuf(f"other{t}", S, F32) for t in range(PACK)]
         sink = [sbuf(f"sink{t}", S, F32) for t in range(PACK)]
+        lift = [sbuf(f"lift{t}", S, F32) for t in range(PACK)]
+        table = [sbuf(f"table{t}", 4 * V, F32) for t in range(PACK)]
+        gain = [moist[:, t * S : (t + 1) * S] for t in range(PACK)]
+
+        for t in range(PACK):
+            for h in range(2):
+                tp = psum.tile([P, BANK], F32, name="bank")
+                product(tp[:], w1d, t, halves[h])
+                nc.scalar.activation(out=temp[t][:, halves[h]], in_=tp[:], func=ACT.Tanh)
+            if t == 0:
+                nc.scalar.activation(out=gain[t], in_=ratio[:], func=ACT.Exp, scale=1.2, bias=-0.6)
+            else:
+                nc.scalar.activation(out=gain[t], in_=gain[t], func=ACT.Tanh, scale=-1.0)
+                nc.scalar.activation(out=gain[t], in_=gain[t], func=ACT.Exp, scale=0.6)
 
         def make_theta(t):
-            temp = sbuf(f"temp{t}", S, F32)
-            for h in range(2):
-                tp = product(w1d, t, h)
-                nc.scalar.activation(out=temp[:, halves[h]], in_=tp[:], func=ACT.Tanh)
-            gain = moist[:, t * S : (t + 1) * S]
-            nc.scalar.activation(out=gain, in_=gain, func=ACT.Tanh, scale=-1.0)
-            nc.scalar.activation(out=gain, in_=gain, func=ACT.Exp, scale=0.6)
-            nc.vector.scalar_tensor_tensor(out=theta[t][:], in0=temp[:], scalar=1.5, in1=gain, op0=ALU.add, op1=ALU.mult)
+            nc.vector.scalar_tensor_tensor(out=theta[t][:], in0=temp[t][:], scalar=1.5, in1=gain[t], op0=ALU.add, op1=ALU.mult)
             if t == 0:
                 nc.vector.tensor_copy(out=other[t][:], in_=theta[t][:])
             if t == 1:
                 nc.sync.dma_start(out=other[t][:], in_=theta[t][:])
+            if t >= 2:
+                for h in range(2):
+                    nc.scalar.activation(out=other[t][:, halves[h]], in_=theta[t][:].indirect(env_t[:, list_halves[h]]), func=ACT.Copy)
 
         def compare(t):
             if t < 2:
                 for h in range(2):
                     nc.vector.tensor_tensor(out=sink[t][:, halves[h]], in0=theta[t][:].indirect(env_t[:, list_halves[h]]), in1=other[t][:, halves[h]], op=ALU.subtract)
             else:
-                for h in range(2):
-                    nc.scalar.activation(out=other[t][:, halves[h]], in_=theta[t][:].indirect(env_t[:, list_halves[h]]), func=ACT.Copy)
                 nc.vector.tensor_tensor(out=sink[t][:], in0=other[t][:], in1=theta[t][:], op=ALU.subtract)
 
-        def integrate(t):
-            table = sbuf(f"table{t}", 4 * V, F32)
-            hid_v, cin, pair = table[:, 0:V], table[:, V : 2 * V], table[:, 2 * V : 4 * V]
+        def energy(t):
+            turned = psum.tile([P, BANK], F32, name="bank")
+            cape_turned = sbuf(f"cape_turned{t}", V, F32)
+            cape = psum.tile([P, BANK], F32, name="bank")
+            pieces = [(0,), (1,)] if t == PACK - 1 else [(0, 1)]
+            for blocks in pieces:
+                cols = slice(blocks[0] * D * P, (blocks[-1] + 1) * D * P)
+                nc.vector.scalar_tensor_tensor(out=lift[t][:, cols], in0=sink[t][:, cols], scalar=0.0, in1=dz_t[:, t, cols], op0=ALU.min, op1=ALU.mult)
+            for b in range(V // P):
+                for d in range(D):
+                    nc.tensor.matmul(turned[:, b * P : (b + 1) * P], lift[t][:, b * D * P + d : (b + 1) * D * P : D], ident[:], is_transpose=True, start=(d == 0), stop=(d == D - 1))
+            nc.scalar.activation(out=cape_turned[:], in_=turned[:, 0:V], func=ACT.Copy, scale=-1.0)
+            for b in range(V // P):
+                nc.tensor.transpose(cape[:, b * P : (b + 1) * P], cape_turned[:, b * P : (b + 1) * P], ident[:])
+            return cape[:, 0:V]
+
+        def inhibition(t):
+            cin, pair = table[t][:, V : 2 * V], table[t][:, 2 * V : 4 * V]
             pair2 = pair.rearrange("p (v e) -> p v e", e=2)
             sink4 = sink[t][:].rearrange("p (v a e) -> p v a e", a=2, e=2)
             nc.vector.tensor_tensor(out=pair2, in0=sink4[:, :, 0, :], in1=sink4[:, :, 1, :], op=ALU.max)
-            lift = sbuf(f"lift{t}", S, F32)
-            nc.vector.scalar_tensor_tensor(out=lift[:], in0=sink[t][:], scalar=0.0, in1=dz_t[:, t, :], op0=ALU.min, op1=ALU.mult)
             nc.vector.scalar_tensor_tensor(out=cin, in0=pair2[:, :, 0], scalar=0.0, in1=pair2[:, :, 1], op0=ALU.max, op1=ALU.max)
             nc.scalar.activation(out=cin, in_=cin, func=ACT.Exp, scale=-1.0)
-            lift4 = lift[:].rearrange("p (v a e) -> p v a e", a=2, e=2)
-            sums = sbuf(f"sums{t}", 2 * V, F32)
-            sums2 = sums[:].rearrange("p (v e) -> p v e", e=2)
-            nc.vector.tensor_tensor(out=sums2, in0=lift4[:, :, 0, :], in1=lift4[:, :, 1, :], op=ALU.add)
-            cape = sbuf(f"cape{t}", V, F32)
-            nc.vector.scalar_tensor_tensor(out=cape[:], in0=sums2[:, :, 0], scalar=-1.0, in1=sums2[:, :, 1], op0=ALU.mult, op1=ALU.subtract)
-            nc.vector.scalar_tensor_tensor(out=hid_v, in0=cape[:], scalar=unit_t[:, t : t + 1], in1=cin, op0=ALU.mult, op1=ALU.mult)
-            nc.scalar.activation(out=planes[:, t, :], in_=table[:].indirect(stn_t[:]), func=ACT.Copy)
+
+        def stations(t, cape):
+            nc.vector.scalar_tensor_tensor(out=table[t][:, 0:V], in0=cape, scalar=unit_t[:, t : t + 1], in1=table[t][:, V : 2 * V], op0=ALU.mult, op1=ALU.mult)
+            pieces = 4 if t == PACK - 1 else 1
+            for c in range(pieces):
+                w = U // pieces
+                nc.scalar.activation(out=planes[:, t, c * w : (c + 1) * w], in_=table[t][:].indirect(stn_t[:, c * w // 16 : (c + 1) * w // 16]), func=ACT.Copy)
 
         make_theta(0)
-        for t in range(PACK):
-            compare(t)
-            if t + 1 < PACK:
-                make_theta(t + 1)
-            integrate(t)
+        compare(0)
+        make_theta(1)
+        cape0 = energy(0)
+        inhibition(0)
+        make_theta(2)
+        compare(1)
+        make_theta(3)
+        cape1 = energy(1)
+        inhibition(1)
+        compare(2)
+        stations(0, cape0)
+        cape2 = energy(2)
+        compare(3)
+        stations(1, cape1)
+        cape3 = energy(3)
+        inhibition(2)
+        inhibition(3)
+        stations(2, cape2)
+        stations(3, cape3)
 
-        half = U // 2
-        for h in range(2):
+        half = U // 4
+        for h in range(4):
             cols = slice(h * half, (h + 1) * half)
             woven = keep.tile([P, half, PACK], BF16, name=f"woven{h}", align_bytes=64)
             nc.vector.tensor_copy(out=woven[:].rearrange("p (c i) t -> p c t i", i=4), in_=planes[:, :, cols].rearrange("p t (c i) -> p c t i", i=4))

@@ -43,7 +43,7 @@ def tile_picked_yweathr_exp_p_kernel(tc, x_words, x_scales, w1_words, w1_scales,
 
         xw = sbuf("xw", T, U32)
         xs = sbuf("xs", T, U8)
-        w2w, w2s = sbuf("w2w", 2 * H, U8, "raw_words"), sbuf("w2s", H, U8, "raw_scales")
+        w2w, w2s = sbuf("w2w", 2 * H, U8), sbuf("w2s", H, U8)
         nc.vector.memset(xs[:].bitcast(I32), 0)
         nc.gpsimd.memset(w2s[:].bitcast(I32), 0)
 
@@ -55,13 +55,13 @@ def tile_picked_yweathr_exp_p_kernel(tc, x_words, x_scales, w1_words, w1_scales,
         load_scale_rows([nc.scalar, nc.scalar, nc.gpsimd, nc.gpsimd], w2s, w2_scales)
         nc.sync.dma_start(stn_t[:], stn)
 
-        def deal_words(engine, name, words):
-            dealt = sbuf(name, 2 * H, U8)
+        def deal_words(engine, name, words, tag=None):
+            dealt = sbuf(name, 2 * H, U8, tag)
             engine.tensor_copy(out=dealt[:].rearrange("p (t m b) -> p t m b", t=PACK, b=2), in_=words[:].rearrange("p (m t b) -> p t m b", t=PACK, b=2))
             return dealt
 
-        def deal_scales(engine, name, scales):
-            dealt = sbuf(name, H, U8)
+        def deal_scales(engine, name, scales, tag=None):
+            dealt = sbuf(name, H, U8, tag)
             engine.tensor_copy(out=dealt[:].rearrange("p (t m) -> p t m", t=PACK), in_=scales[:].rearrange("p (m t) -> p t m", t=PACK))
             return dealt
 
@@ -79,19 +79,12 @@ def tile_picked_yweathr_exp_p_kernel(tc, x_words, x_scales, w1_words, w1_scales,
         for q in range(1, 4):
             pick(xgs, xs, q)
             pick(xgw, xw, q)
-        w1w, w1s = sbuf("w1w", 2 * H, U8, "raw_words"), sbuf("w1s", H, U8, "raw_scales")
-        nc.gpsimd.memset(w1s[:].bitcast(I32), 0)
+        w1w, w1s = sbuf("w1w", 2 * H, U8, "w2w"), sbuf("w1s", H, U8, "w2s")
         nc.sync.dma_start(out=w1w[:].bitcast(I32), in_=w1_words[0].bitcast(I32))
+        nc.gpsimd.memset(w1s[:].bitcast(I32), 0)
         load_scale_rows([nc.sync] * 4, w1s, w1_scales)
-        w1d = (deal_words(nc.gpsimd, "w1_dw", w1w), deal_scales(nc.gpsimd, "w1_ds", w1s))
-        w3w, w3s = sbuf("w3w", 2 * N, U8, "raw_words"), sbuf("w3s", N, U8, "raw_scales")
-        nc.gpsimd.memset(w3s[:].bitcast(I32), 0)
-        nc.sync.dma_start(out=w3w[:].bitcast(I32), in_=w3_words[0].bitcast(I32))
-        load_scale_rows([nc.sync] * 4, w3s, w3_scales)
         dz_t = keep.tile([P, PACK, S], F32, name="dz_t", tag="xw", align_bytes=64)
         nc.sync.dma_start(out=dz_t[:], in_=dz.rearrange("(p t) j -> p t j", t=PACK))
-        unit_t = sbuf("unit_t", PACK, F32, "xs")
-        nc.sync.dma_start(out=unit_t[:], in_=unit.rearrange("(p t) o -> p (t o)", t=PACK))
 
         def product(acc, wd, t, cols):
             nc.tensor.matmul_mx(out=acc, lhsT=wd[0][:, 2 * P * t : 2 * P * (t + 1)].bitcast(FP4X4), lhsT_scale=wd[1][:, P * t : P * (t + 1)],
@@ -107,11 +100,20 @@ def tile_picked_yweathr_exp_p_kernel(tc, x_words, x_scales, w1_words, w1_scales,
                     product(wv[:, e, :], w2d, 2 * u + e, cols)
                 nc.scalar.activation(out=moist3[:, 2 * u : 2 * u + 2, cols], in_=wv[:], func=ACT.Sigmoid, scale=-1.0)
         ratio = sbuf("ratio", S, F32)
+        square = [sbuf(f"square{h}", BANK, F32) for h in range(2)]
         for h in range(2):
-            nc.vector.tensor_tensor(out=ratio[:, halves[h]], in0=moist[:, halves[h]], in1=moist[:, halves[h]], op=ALU.mult)
+            nc.vector.tensor_tensor(out=square[h][:], in0=moist[:, halves[h]], in1=moist[:, halves[h]], op=ALU.mult)
         for h in range(2):
-            nc.vector.tensor_scalar_add(out=ratio[:, halves[h]], in0=ratio[:, halves[h]], scalar1=1.0)
-        nc.vector.reciprocal(out=ratio[:], in_=ratio[:])
+            nc.vector.tensor_scalar_add(out=ratio[:, halves[h]], in0=square[h][:], scalar1=1.0)
+        for h in range(2):
+            nc.vector.reciprocal(out=ratio[:, halves[h]], in_=ratio[:, halves[h]])
+        w1d = (deal_words(nc.gpsimd, "w1_dw", w1w, "square0"), deal_scales(nc.gpsimd, "w1_ds", w1s, "square1"))
+        w3w, w3s = sbuf("w3w", 2 * N, U8, "w2w"), sbuf("w3s", N, U8, "w2s")
+        nc.gpsimd.memset(w3s[:].bitcast(I32), 0)
+        nc.sync.dma_start(out=w3w[:].bitcast(I32), in_=w3_words[0].bitcast(I32))
+        load_scale_rows([nc.sync] * 4, w3s, w3_scales)
+        unit_t = sbuf("unit_t", PACK, F32, "xs")
+        nc.sync.dma_start(out=unit_t[:], in_=unit.rearrange("(p t) o -> p (t o)", t=PACK))
         nc.scalar.activation(out=moist[:, S:], in_=moist[:, S:], func=ACT.Ln, bias=LN_FLOOR)
 
         ident = sbuf("ident", P, F32)
@@ -119,28 +121,30 @@ def tile_picked_yweathr_exp_p_kernel(tc, x_words, x_scales, w1_words, w1_scales,
 
         planes = keep.tile([P, PACK, U], BF16, name="planes", align_bytes=64)
         temp = [sbuf(f"temp{t}", S, F32) for t in range(PACK)]
+        gain = [sbuf(f"gain{t}", S, F32) for t in range(PACK)]
         theta = [sbuf(f"theta{t}", S, F32) for t in range(PACK)]
         other = [sbuf(f"other{t}", S, F32) for t in range(PACK)]
         sink = [sbuf(f"sink{t}", S, F32) for t in range(PACK)]
-        lift = [sbuf(f"lift{t}", S, F32) for t in range(PACK)]
-        table = [sbuf(f"table{t}", 4 * V, F32) for t in range(PACK)]
-        gain = [moist[:, t * S : (t + 1) * S] for t in range(PACK)]
 
         for t in range(PACK):
+            logged = moist[:, t * S : (t + 1) * S]
+            if t > 0:
+                nc.scalar.activation(out=logged, in_=logged, func=ACT.Tanh, scale=-1.0)
             for h in range(2):
                 tp = psum.tile([P, BANK], F32, name="bank")
                 product(tp[:], w1d, t, halves[h])
                 nc.scalar.activation(out=temp[t][:, halves[h]], in_=tp[:], func=ACT.Tanh)
-            if t == 0:
-                nc.scalar.activation(out=gain[t], in_=ratio[:], func=ACT.Exp, scale=1.2, bias=-0.6)
-            else:
-                nc.scalar.activation(out=gain[t], in_=gain[t], func=ACT.Tanh, scale=-1.0)
-                nc.scalar.activation(out=gain[t], in_=gain[t], func=ACT.Exp, scale=0.6)
+                if t == 0:
+                    nc.scalar.activation(out=gain[t][:, halves[h]], in_=ratio[:, halves[h]], func=ACT.Exp, scale=1.2, bias=-0.6)
+            if t > 0:
+                nc.scalar.activation(out=gain[t][:], in_=logged, func=ACT.Exp, scale=0.6)
 
         def make_theta(t):
-            nc.vector.scalar_tensor_tensor(out=theta[t][:], in0=temp[t][:], scalar=1.5, in1=gain[t], op0=ALU.add, op1=ALU.mult)
+            for cols in halves if t == 0 else [slice(0, S)]:
+                nc.vector.scalar_tensor_tensor(out=theta[t][:, cols], in0=temp[t][:, cols], scalar=1.5, in1=gain[t][:, cols], op0=ALU.add, op1=ALU.mult)
             if t == 0:
-                nc.vector.tensor_copy(out=other[t][:], in_=theta[t][:])
+                for cols in halves:
+                    nc.vector.tensor_copy(out=other[t][:, cols], in_=theta[t][:, cols])
             if t == 1:
                 nc.sync.dma_start(out=other[t][:], in_=theta[t][:])
             if t >= 2:
@@ -154,57 +158,68 @@ def tile_picked_yweathr_exp_p_kernel(tc, x_words, x_scales, w1_words, w1_scales,
             else:
                 nc.vector.tensor_tensor(out=sink[t][:], in0=other[t][:], in1=theta[t][:], op=ALU.subtract)
 
-        def energy(t):
+        def energy(t, tag=None):
+            lift = sbuf(f"lift{t}", S, F32, tag)
+            nc.vector.scalar_tensor_tensor(out=lift[:], in0=sink[t][:], scalar=0.0, in1=dz_t[:, t, :], op0=ALU.min, op1=ALU.mult)
+            if t == PACK - 1:
+                lift4 = lift[:].rearrange("p (v a e) -> p v a e", a=2, e=2)
+                sums = sbuf("sums", 2 * V, F32)
+                sums2 = sums[:].rearrange("p (v e) -> p v e", e=2)
+                nc.vector.tensor_tensor(out=sums2, in0=lift4[:, :, 0, :], in1=lift4[:, :, 1, :], op=ALU.add)
+                cape = sbuf("cape", V, F32)
+                nc.vector.scalar_tensor_tensor(out=cape[:], in0=sums2[:, :, 0], scalar=-1.0, in1=sums2[:, :, 1], op0=ALU.mult, op1=ALU.subtract)
+                return cape[:]
             turned = psum.tile([P, BANK], F32, name="bank")
             cape_turned = sbuf(f"cape_turned{t}", V, F32)
             cape = psum.tile([P, BANK], F32, name="bank")
-            pieces = [(0,), (1,)] if t == PACK - 1 else [(0, 1)]
-            for blocks in pieces:
-                cols = slice(blocks[0] * D * P, (blocks[-1] + 1) * D * P)
-                nc.vector.scalar_tensor_tensor(out=lift[t][:, cols], in0=sink[t][:, cols], scalar=0.0, in1=dz_t[:, t, cols], op0=ALU.min, op1=ALU.mult)
             for b in range(V // P):
                 for d in range(D):
-                    nc.tensor.matmul(turned[:, b * P : (b + 1) * P], lift[t][:, b * D * P + d : (b + 1) * D * P : D], ident[:], is_transpose=True, start=(d == 0), stop=(d == D - 1))
+                    nc.tensor.matmul(turned[:, b * P : (b + 1) * P], lift[:, b * D * P + d : (b + 1) * D * P : D], ident[:], is_transpose=True, start=(d == 0), stop=(d == D - 1))
             nc.scalar.activation(out=cape_turned[:], in_=turned[:, 0:V], func=ACT.Copy, scale=-1.0)
             for b in range(V // P):
                 nc.tensor.transpose(cape[:, b * P : (b + 1) * P], cape_turned[:, b * P : (b + 1) * P], ident[:])
             return cape[:, 0:V]
 
-        def inhibition(t):
-            cin, pair = table[t][:, V : 2 * V], table[t][:, 2 * V : 4 * V]
-            pair2 = pair.rearrange("p (v e) -> p v e", e=2)
+        def inhibition(t, tag=None):
+            work = sbuf(f"work{t}", 3 * V, F32, tag)
+            cin, pair2 = work[:, 0:V], work[:, V : 3 * V].rearrange("p (v e) -> p v e", e=2)
             sink4 = sink[t][:].rearrange("p (v a e) -> p v a e", a=2, e=2)
             nc.vector.tensor_tensor(out=pair2, in0=sink4[:, :, 0, :], in1=sink4[:, :, 1, :], op=ALU.max)
             nc.vector.scalar_tensor_tensor(out=cin, in0=pair2[:, :, 0], scalar=0.0, in1=pair2[:, :, 1], op0=ALU.max, op1=ALU.max)
             nc.scalar.activation(out=cin, in_=cin, func=ACT.Exp, scale=-1.0)
+            return cin
 
-        def stations(t, cape):
-            nc.vector.scalar_tensor_tensor(out=table[t][:, 0:V], in0=cape, scalar=unit_t[:, t : t + 1], in1=table[t][:, V : 2 * V], op0=ALU.mult, op1=ALU.mult)
-            pieces = 4 if t == PACK - 1 else 1
-            for c in range(pieces):
-                w = U // pieces
-                nc.scalar.activation(out=planes[:, t, c * w : (c + 1) * w], in_=table[t][:].indirect(stn_t[:, c * w // 16 : (c + 1) * w // 16]), func=ACT.Copy)
+        def stations(t, cape, damp, tag=None):
+            table = sbuf(f"table{t}", V, F32, tag)
+            nc.vector.scalar_tensor_tensor(out=table[:], in0=cape, scalar=unit_t[:, t : t + 1], in1=damp, op0=ALU.mult, op1=ALU.mult)
+            w = U // 4
+            for c in range(4):
+                dst, src = planes[:, t, c * w : (c + 1) * w], table[:].indirect(stn_t[:, c * w // 16 : (c + 1) * w // 16])
+                if t == PACK - 1 and c < 2:
+                    nc.vector.tensor_copy(out=dst, in_=src)
+                else:
+                    nc.scalar.activation(out=dst, in_=src, func=ACT.Copy)
 
         make_theta(0)
         compare(0)
         make_theta(1)
-        cape0 = energy(0)
-        inhibition(0)
+        cape0 = energy(0, "temp1")
+        damp0 = inhibition(0, "gain1")
         make_theta(2)
         compare(1)
         make_theta(3)
-        cape1 = energy(1)
-        inhibition(1)
+        cape1 = energy(1, "temp3")
+        damp1 = inhibition(1, "gain3")
         compare(2)
-        stations(0, cape0)
         cape2 = energy(2)
+        stations(0, cape0, damp0, "other2")
         compare(3)
-        stations(1, cape1)
+        stations(1, cape1, damp1, "other3")
+        damp2 = inhibition(2)
         cape3 = energy(3)
-        inhibition(2)
-        inhibition(3)
-        stations(2, cape2)
-        stations(3, cape3)
+        damp3 = inhibition(3)
+        stations(2, cape2, damp2)
+        stations(3, cape3, damp3)
 
         half = U // 4
         for h in range(4):

@@ -19,28 +19,50 @@ ALU = mybir.AluOpType
 
 P = 128
 PACK = 4
+LAST = PACK - 1
 BANK = 512
-LN_FLOOR = 2.0 ** -60
+BANKS = 8
+PER_COLUMN = 16
 QUARTER = S // 4
+PIECE = U // 4
+FUSED_TILES = 2
+VECTOR_PIECES = 2
+LN_FLOOR = 2.0 ** -60
 
 
 def tile_picked_yweathr_exp_p_kernel(tc, x_words, x_scales, w1_words, w1_scales, w2_words, w2_scales, dz, unit, w3_words, w3_scales, offs, env, stn, out):
     nc = tc.nc
     with ExitStack() as ctx:
         keep = ctx.enter_context(tc.tile_pool(name="keep", bufs=1))
-        psum = ctx.enter_context(tc.psum_pool(name="psum", bufs=8))
+        psum = ctx.enter_context(tc.psum_pool(name="psum", bufs=BANKS))
 
-        def sbuf(name, width, dtype, tag=None):
-            return keep.tile([P, width], dtype, name=name, tag=tag or name, align_bytes=64)
+        def sbuf(name, width, dtype, after=None):
+            return keep.tile([P, width], dtype, name=name, tag=after or name, align_bytes=64)
 
-        def load_scale_rows(queues, plane, scales):
+        def entries(list_tile, cols):
+            return list_tile[:, cols.start // PER_COLUMN : cols.stop // PER_COLUMN]
+
+        def load_scale_rows(queues, scale_tile, scales):
             for q in range(4):
-                queues[q].dma_start(out=plane[32 * q : 32 * q + 4, :].bitcast(I32), in_=scales[0, 4 * q : 4 * q + 4, :].bitcast(I32))
+                queues[q].dma_start(out=scale_tile[32 * q : 32 * q + 4, :].bitcast(I32), in_=scales[0, 4 * q : 4 * q + 4, :].bitcast(I32))
 
-        offs_t = keep.tile([P, S // 16], U16, name="offs_t")
-        env_t = keep.tile([P, S // 16], U16, name="env_t")
-        stn_t = keep.tile([P, U // 16], U16, name="stn_t")
+        def deal_words(engine, name, words, after=None):
+            dealt = sbuf(name, 2 * H, U8, after)
+            engine.tensor_copy(out=dealt[:].rearrange("p (t m b) -> p t m b", t=PACK, b=2), in_=words[:].rearrange("p (m t b) -> p t m b", t=PACK, b=2))
+            return dealt
 
+        def deal_scales(engine, name, scales, after=None):
+            dealt = sbuf(name, H, U8, after)
+            engine.tensor_copy(out=dealt[:].rearrange("p (t m) -> p t m", t=PACK), in_=scales[:].rearrange("p (m t) -> p t m", t=PACK))
+            return dealt
+
+        halves = [slice(h * BANK, (h + 1) * BANK) for h in range(S // BANK)]
+        quarters = [slice(q * QUARTER, (q + 1) * QUARTER) for q in range(S // QUARTER)]
+        pieces = [slice(c * PIECE, (c + 1) * PIECE) for c in range(U // PIECE)]
+
+        offs_t = keep.tile([P, S // PER_COLUMN], U16, name="offs_t")
+        env_t = keep.tile([P, S // PER_COLUMN], U16, name="env_t")
+        stn_t = keep.tile([P, U // PER_COLUMN], U16, name="stn_t")
         xw = sbuf("xw", T, U32)
         xs = sbuf("xs", T, U8)
         w2w, w2s = sbuf("w2w", 2 * H, U8), sbuf("w2s", H, U8)
@@ -55,119 +77,110 @@ def tile_picked_yweathr_exp_p_kernel(tc, x_words, x_scales, w1_words, w1_scales,
         load_scale_rows([nc.scalar, nc.scalar, nc.gpsimd, nc.gpsimd], w2s, w2_scales)
         nc.sync.dma_start(stn_t[:], stn)
 
-        def deal_words(engine, name, words, tag=None):
-            dealt = sbuf(name, 2 * H, U8, tag)
-            engine.tensor_copy(out=dealt[:].rearrange("p (t m b) -> p t m b", t=PACK, b=2), in_=words[:].rearrange("p (m t b) -> p t m b", t=PACK, b=2))
-            return dealt
+        picked_words, picked_scales = sbuf("picked_words", S, U32), sbuf("picked_scales", S, U8)
 
-        def deal_scales(engine, name, scales, tag=None):
-            dealt = sbuf(name, H, U8, tag)
-            engine.tensor_copy(out=dealt[:].rearrange("p (t m) -> p t m", t=PACK), in_=scales[:].rearrange("p (m t) -> p t m", t=PACK))
-            return dealt
+        def pick(cols):
+            nc.vector.tensor_copy(out=picked_scales[:, cols], in_=xs[:].indirect(entries(offs_t, cols)))
+            nc.vector.tensor_copy(out=picked_words[:, cols], in_=xw[:].indirect(entries(offs_t, cols)))
 
-        halves = [slice(h * BANK, (h + 1) * BANK) for h in range(S // BANK)]
-        list_halves = [slice(h * BANK // 16, (h + 1) * BANK // 16) for h in range(S // BANK)]
-        xgw, xgs = sbuf("xgw", S, U32), sbuf("xgs", S, U8)
+        w2_dealt_words = deal_words(nc.vector, "w2_dealt_words", w2w)
+        pick(quarters[0])
+        w2_dealt = (w2_dealt_words, deal_scales(nc.gpsimd, "w2_dealt_scales", w2s))
+        for cols in quarters[1:]:
+            pick(cols)
 
-        def pick(dst, src, q):
-            nc.vector.tensor_copy(out=dst[:, q * QUARTER : (q + 1) * QUARTER], in_=src[:].indirect(offs_t[:, q * QUARTER // 16 : (q + 1) * QUARTER // 16]))
-
-        w2_dw = deal_words(nc.vector, "w2_dw", w2w)
-        pick(xgs, xs, 0)
-        pick(xgw, xw, 0)
-        w2d = (w2_dw, deal_scales(nc.vector, "w2_ds", w2s))
-        for q in range(1, 4):
-            pick(xgs, xs, q)
-            pick(xgw, xw, q)
-        w1w, w1s = sbuf("w1w", 2 * H, U8, "w2w"), sbuf("w1s", H, U8, "w2s")
+        w1w, w1s = sbuf("w1w", 2 * H, U8, after="w2w"), sbuf("w1s", H, U8, after="w2s")
         nc.sync.dma_start(out=w1w[:].bitcast(I32), in_=w1_words[0].bitcast(I32))
         nc.gpsimd.memset(w1s[:].bitcast(I32), 0)
         load_scale_rows([nc.sync] * 4, w1s, w1_scales)
         dz_t = keep.tile([P, PACK, S], F32, name="dz_t", tag="xw", align_bytes=64)
         nc.sync.dma_start(out=dz_t[:], in_=dz.rearrange("(p t) j -> p t j", t=PACK))
 
-        def product(acc, wd, t, cols):
-            nc.tensor.matmul_mx(out=acc, lhsT=wd[0][:, 2 * P * t : 2 * P * (t + 1)].bitcast(FP4X4), lhsT_scale=wd[1][:, P * t : P * (t + 1)],
-                                rhs=xgw[:, cols].bitcast(FP8X4), rhs_scale=xgs[:, cols], start=True, stop=True)
+        def product(acc, dealt, t, cols):
+            words, scales = dealt
+            nc.tensor.matmul_mx(out=acc, lhsT=words[:, 2 * P * t : 2 * P * (t + 1)].bitcast(FP4X4), lhsT_scale=scales[:, P * t : P * (t + 1)],
+                                rhs=picked_words[:, cols].bitcast(FP8X4), rhs_scale=picked_scales[:, cols], start=True, stop=True)
 
         moist = sbuf("moist", PACK * S, F32)
-        moist3 = moist[:].rearrange("p (t j) -> p t j", t=PACK)
-        for q in range(4):
-            cols = slice(q * QUARTER, (q + 1) * QUARTER)
-            for u in range(2):
+        moist_by_tile = moist[:].rearrange("p (t j) -> p t j", t=PACK)
+        for cols in quarters:
+            for t0 in range(0, PACK, 2):
                 wv = psum.tile([P, 2, QUARTER], F32, name="bank")
                 for e in range(2):
-                    product(wv[:, e, :], w2d, 2 * u + e, cols)
-                nc.scalar.activation(out=moist3[:, 2 * u : 2 * u + 2, cols], in_=wv[:], func=ACT.Sigmoid, scale=-1.0)
+                    product(wv[:, e, :], w2_dealt, t0 + e, cols)
+                nc.scalar.activation(out=moist_by_tile[:, t0 : t0 + 2, cols], in_=wv[:], func=ACT.Sigmoid, scale=-1.0)
+
         ratio = sbuf("ratio", S, F32)
-        square = [sbuf(f"square{h}", BANK, F32) for h in range(2)]
-        for h in range(2):
-            nc.vector.tensor_tensor(out=square[h][:], in0=moist[:, halves[h]], in1=moist[:, halves[h]], op=ALU.mult)
-        for h in range(2):
-            nc.vector.tensor_scalar_add(out=ratio[:, halves[h]], in0=square[h][:], scalar1=1.0)
-        for h in range(2):
-            nc.vector.reciprocal(out=ratio[:, halves[h]], in_=ratio[:, halves[h]])
-        w1d = (deal_words(nc.gpsimd, "w1_dw", w1w, "square0"), deal_scales(nc.gpsimd, "w1_ds", w1s, "square1"))
-        w3w, w3s = sbuf("w3w", 2 * N, U8, "w2w"), sbuf("w3s", N, U8, "w2s")
+        square = [sbuf(f"square{h}", BANK, F32) for h in range(len(halves))]
+        for h, cols in enumerate(halves):
+            nc.vector.tensor_tensor(out=square[h][:], in0=moist[:, cols], in1=moist[:, cols], op=ALU.mult)
+        for h, cols in enumerate(halves):
+            nc.vector.tensor_scalar_add(out=ratio[:, cols], in0=square[h][:], scalar1=1.0)
+        for cols in halves:
+            nc.vector.reciprocal(out=ratio[:, cols], in_=ratio[:, cols])
+        w1_dealt = (deal_words(nc.gpsimd, "w1_dealt_words", w1w, after="square0"), deal_scales(nc.gpsimd, "w1_dealt_scales", w1s, after="square1"))
+        w3w, w3s = sbuf("w3w", 2 * N, U8, after="w2w"), sbuf("w3s", N, U8, after="w2s")
         nc.gpsimd.memset(w3s[:].bitcast(I32), 0)
         nc.sync.dma_start(out=w3w[:].bitcast(I32), in_=w3_words[0].bitcast(I32))
         load_scale_rows([nc.sync] * 4, w3s, w3_scales)
-        unit_t = sbuf("unit_t", PACK, F32, "xs")
+        unit_t = sbuf("unit_t", PACK, F32, after="xs")
         nc.sync.dma_start(out=unit_t[:], in_=unit.rearrange("(p t) o -> p (t o)", t=PACK))
         nc.scalar.activation(out=moist[:, S:], in_=moist[:, S:], func=ACT.Ln, bias=LN_FLOOR)
 
         ident = sbuf("ident", P, F32)
         make_identity(nc, ident[:])
 
-        planes = keep.tile([P, PACK, U], BF16, name="planes", align_bytes=64)
+        hid = keep.tile([P, PACK, U], BF16, name="hid", align_bytes=64)
         temp = [sbuf(f"temp{t}", S, F32) for t in range(PACK)]
         gain = [sbuf(f"gain{t}", S, F32) for t in range(PACK)]
         theta = [sbuf(f"theta{t}", S, F32) for t in range(PACK)]
-        other = [sbuf(f"other{t}", S, F32) for t in range(PACK)]
+        partner = [sbuf(f"partner{t}", S, F32) for t in range(PACK)]
         sink = [sbuf(f"sink{t}", S, F32) for t in range(PACK)]
 
+        first_tile_steps = [[halves[0]], quarters[2:]]
         for t in range(PACK):
-            logged = moist[:, t * S : (t + 1) * S]
+            tile_moist = moist[:, t * S : (t + 1) * S]
             if t > 0:
-                nc.scalar.activation(out=logged, in_=logged, func=ACT.Tanh, scale=-1.0)
-            for h in range(2):
+                nc.scalar.activation(out=tile_moist, in_=tile_moist, func=ACT.Tanh, scale=-1.0)
+            for h, cols in enumerate(halves):
                 tp = psum.tile([P, BANK], F32, name="bank")
-                product(tp[:], w1d, t, halves[h])
-                nc.scalar.activation(out=temp[t][:, halves[h]], in_=tp[:], func=ACT.Tanh)
+                product(tp[:], w1_dealt, t, cols)
+                nc.scalar.activation(out=temp[t][:, cols], in_=tp[:], func=ACT.Tanh)
                 if t == 0:
-                    nc.scalar.activation(out=gain[t][:, halves[h]], in_=ratio[:, halves[h]], func=ACT.Exp, scale=1.2, bias=-0.6)
+                    for step in first_tile_steps[h]:
+                        nc.scalar.activation(out=gain[t][:, step], in_=ratio[:, step], func=ACT.Exp, scale=1.2, bias=-0.6)
             if t > 0:
-                nc.scalar.activation(out=gain[t][:], in_=logged, func=ACT.Exp, scale=0.6)
+                nc.scalar.activation(out=gain[t][:], in_=tile_moist, func=ACT.Exp, scale=0.6)
 
         def make_theta(t):
-            for cols in halves if t == 0 else [slice(0, S)]:
+            for cols in first_tile_steps[0] + first_tile_steps[1] if t == 0 else [slice(0, S)]:
                 nc.vector.scalar_tensor_tensor(out=theta[t][:, cols], in0=temp[t][:, cols], scalar=1.5, in1=gain[t][:, cols], op0=ALU.add, op1=ALU.mult)
             if t == 0:
                 for cols in halves:
-                    nc.vector.tensor_copy(out=other[t][:, cols], in_=theta[t][:, cols])
-            if t == 1:
-                nc.sync.dma_start(out=other[t][:], in_=theta[t][:])
-            if t >= 2:
-                for h in range(2):
-                    nc.scalar.activation(out=other[t][:, halves[h]], in_=theta[t][:].indirect(env_t[:, list_halves[h]]), func=ACT.Copy)
+                    nc.vector.tensor_copy(out=partner[t][:, cols], in_=theta[t][:, cols])
+            elif t < FUSED_TILES:
+                nc.sync.dma_start(out=partner[t][:], in_=theta[t][:])
+            else:
+                for cols in halves:
+                    nc.scalar.activation(out=partner[t][:, cols], in_=theta[t][:].indirect(entries(env_t, cols)), func=ACT.Copy)
 
         def compare(t):
-            if t < 2:
-                for h in range(2):
-                    nc.vector.tensor_tensor(out=sink[t][:, halves[h]], in0=theta[t][:].indirect(env_t[:, list_halves[h]]), in1=other[t][:, halves[h]], op=ALU.subtract)
+            if t < FUSED_TILES:
+                for cols in halves:
+                    nc.vector.tensor_tensor(out=sink[t][:, cols], in0=theta[t][:].indirect(entries(env_t, cols)), in1=partner[t][:, cols], op=ALU.subtract)
             else:
-                nc.vector.tensor_tensor(out=sink[t][:], in0=other[t][:], in1=theta[t][:], op=ALU.subtract)
+                nc.vector.tensor_tensor(out=sink[t][:], in0=partner[t][:], in1=theta[t][:], op=ALU.subtract)
 
-        def energy(t, tag=None):
-            lift = sbuf(f"lift{t}", S, F32, tag)
+        def energy(t, after=None):
+            lift = sbuf(f"lift{t}", S, F32, after)
             nc.vector.scalar_tensor_tensor(out=lift[:], in0=sink[t][:], scalar=0.0, in1=dz_t[:, t, :], op0=ALU.min, op1=ALU.mult)
-            if t == PACK - 1:
-                lift4 = lift[:].rearrange("p (v a e) -> p v a e", a=2, e=2)
+            if t == LAST:
+                levels = lift[:].rearrange("p (v a e) -> p v a e", a=2, e=2)
                 sums = sbuf("sums", 2 * V, F32)
-                sums2 = sums[:].rearrange("p (v e) -> p v e", e=2)
-                nc.vector.tensor_tensor(out=sums2, in0=lift4[:, :, 0, :], in1=lift4[:, :, 1, :], op=ALU.add)
+                pair_sums = sums[:].rearrange("p (v e) -> p v e", e=2)
+                nc.vector.tensor_tensor(out=pair_sums, in0=levels[:, :, 0, :], in1=levels[:, :, 1, :], op=ALU.add)
                 cape = sbuf("cape", V, F32)
-                nc.vector.scalar_tensor_tensor(out=cape[:], in0=sums2[:, :, 0], scalar=-1.0, in1=sums2[:, :, 1], op0=ALU.mult, op1=ALU.subtract)
+                nc.vector.scalar_tensor_tensor(out=cape[:], in0=pair_sums[:, :, 0], scalar=-1.0, in1=pair_sums[:, :, 1], op0=ALU.mult, op1=ALU.subtract)
                 return cape[:]
             turned = psum.tile([P, BANK], F32, name="bank")
             cape_turned = sbuf(f"cape_turned{t}", V, F32)
@@ -180,56 +193,53 @@ def tile_picked_yweathr_exp_p_kernel(tc, x_words, x_scales, w1_words, w1_scales,
                 nc.tensor.transpose(cape[:, b * P : (b + 1) * P], cape_turned[:, b * P : (b + 1) * P], ident[:])
             return cape[:, 0:V]
 
-        def inhibition(t, tag=None):
-            work = sbuf(f"work{t}", 3 * V, F32, tag)
-            cin, pair2 = work[:, 0:V], work[:, V : 3 * V].rearrange("p (v e) -> p v e", e=2)
-            sink4 = sink[t][:].rearrange("p (v a e) -> p v a e", a=2, e=2)
-            nc.vector.tensor_tensor(out=pair2, in0=sink4[:, :, 0, :], in1=sink4[:, :, 1, :], op=ALU.max)
-            nc.vector.scalar_tensor_tensor(out=cin, in0=pair2[:, :, 0], scalar=0.0, in1=pair2[:, :, 1], op0=ALU.max, op1=ALU.max)
+        def inhibition(t, after=None):
+            work = sbuf(f"work{t}", 3 * V, F32, after)
+            cin, pair_max = work[:, 0:V], work[:, V : 3 * V].rearrange("p (v e) -> p v e", e=2)
+            levels = sink[t][:].rearrange("p (v a e) -> p v a e", a=2, e=2)
+            nc.vector.tensor_tensor(out=pair_max, in0=levels[:, :, 0, :], in1=levels[:, :, 1, :], op=ALU.max)
+            nc.vector.scalar_tensor_tensor(out=cin, in0=pair_max[:, :, 0], scalar=0.0, in1=pair_max[:, :, 1], op0=ALU.max, op1=ALU.max)
             nc.scalar.activation(out=cin, in_=cin, func=ACT.Exp, scale=-1.0)
             return cin
 
-        def stations(t, cape, damp, tag=None):
-            table = sbuf(f"table{t}", V, F32, tag)
+        def stations(t, cape, damp, after=None):
+            table = sbuf(f"table{t}", V, F32, after)
             nc.vector.scalar_tensor_tensor(out=table[:], in0=cape, scalar=unit_t[:, t : t + 1], in1=damp, op0=ALU.mult, op1=ALU.mult)
-            w = U // 4
-            for c in range(4):
-                dst, src = planes[:, t, c * w : (c + 1) * w], table[:].indirect(stn_t[:, c * w // 16 : (c + 1) * w // 16])
-                if t == PACK - 1 and c < 2:
-                    nc.vector.tensor_copy(out=dst, in_=src)
+            for c, cols in enumerate(pieces):
+                looked_up = table[:].indirect(entries(stn_t, cols))
+                if t == LAST and c < VECTOR_PIECES:
+                    nc.vector.tensor_copy(out=hid[:, t, cols], in_=looked_up)
                 else:
-                    nc.scalar.activation(out=dst, in_=src, func=ACT.Copy)
+                    nc.scalar.activation(out=hid[:, t, cols], in_=looked_up, func=ACT.Copy)
 
         make_theta(0)
         compare(0)
         make_theta(1)
-        cape0 = energy(0, "temp1")
-        damp0 = inhibition(0, "gain1")
+        cape0 = energy(0, after="temp1")
+        damp0 = inhibition(0, after="gain1")
         make_theta(2)
         compare(1)
         make_theta(3)
-        cape1 = energy(1, "temp3")
-        damp1 = inhibition(1, "gain3")
+        cape1 = energy(1, after="temp3")
+        damp1 = inhibition(1, after="gain3")
         compare(2)
         cape2 = energy(2)
-        stations(0, cape0, damp0, "other2")
+        stations(0, cape0, damp0, after="partner2")
         compare(3)
-        stations(1, cape1, damp1, "other3")
+        stations(1, cape1, damp1, after="partner3")
         damp2 = inhibition(2)
         cape3 = energy(3)
         damp3 = inhibition(3)
         stations(2, cape2, damp2)
         stations(3, cape3, damp3)
 
-        half = U // 4
-        for h in range(4):
-            cols = slice(h * half, (h + 1) * half)
-            woven = keep.tile([P, half, PACK], BF16, name=f"woven{h}", align_bytes=64)
-            nc.vector.tensor_copy(out=woven[:].rearrange("p (c i) t -> p c t i", i=4), in_=planes[:, :, cols].rearrange("p t (c i) -> p c t i", i=4))
-            codes, scales = sbuf(f"codes{h}", half, U32), sbuf(f"scales{h}", half, U8)
-            nc.vector.quantize_mx(out=codes[:].bitcast(FP8X4), scales=scales[:], in_=woven[:].rearrange("p c t -> p (c t)"))
+        for c, cols in enumerate(pieces):
+            woven = keep.tile([P, PIECE, PACK], BF16, name=f"woven{c}", align_bytes=64)
+            nc.vector.tensor_copy(out=woven[:].rearrange("p (g i) t -> p g t i", i=4), in_=hid[:, :, cols].rearrange("p t (g i) -> p g t i", i=4))
+            hid_words, hid_scales = sbuf(f"hid_words{c}", PIECE, U32), sbuf(f"hid_scales{c}", PIECE, U8)
+            nc.vector.quantize_mx(out=hid_words[:].bitcast(FP8X4), scales=hid_scales[:], in_=woven[:].rearrange("p r t -> p (r t)"))
             acc = psum.tile([P, BANK], F32, name="bank")
-            nc.tensor.matmul_mx(out=acc[:, 0:half], lhsT=w3w[:].bitcast(FP4X4), lhsT_scale=w3s[:], rhs=codes[:].bitcast(FP8X4), rhs_scale=scales[:], start=True, stop=True)
-            res = sbuf(f"res{h}", half, F32)
-            nc.scalar.copy(out=res[:], in_=acc[:, 0:half])
-            nc.sync.dma_start(out=out[:, cols], in_=res[:])
+            nc.tensor.matmul_mx(out=acc[:, 0:PIECE], lhsT=w3w[:].bitcast(FP4X4), lhsT_scale=w3s[:], rhs=hid_words[:].bitcast(FP8X4), rhs_scale=hid_scales[:], start=True, stop=True)
+            result = sbuf(f"result{c}", PIECE, F32)
+            nc.scalar.copy(out=result[:], in_=acc[:, 0:PIECE])
+            nc.sync.dma_start(out=out[:, cols], in_=result[:])

from contextlib import ExitStack

import concourse.mybir as mybir
from concourse.masks import make_identity

K, T, S, D, N, H, V, U = 512, 2048, 1024, 4, 128, 512, 256, 512
FLOPS = 2 * (2 * K * H * S) + 2 * H * N * U

F32 = mybir.dt.float32
BF16 = mybir.dt.bfloat16
I32 = mybir.dt.int32
U32 = mybir.dt.uint32
U16 = mybir.dt.uint16
U8 = mybir.dt.uint8
FP8X4 = mybir.dt.float8_e4m3fn_x4
FP4X4 = mybir.dt.float4_e2m1fn_x4
ACT = mybir.ActivationFunctionType
ALU = mybir.AluOpType

P = 128
PACK = 4
LAST = PACK - 1
BANK = 512
BANKS = 8
PER_COLUMN = 16
QUARTER = S // 4
PIECE = U // 4
FUSED_TILES = 2
VECTOR_PIECES = 2
LN_FLOOR = 2.0 ** -60


def tile_picked_yweathr_exp_p_kernel(tc, x_words, x_scales, w1_words, w1_scales, w2_words, w2_scales, dz, unit, w3_words, w3_scales, offs, env, stn, out):
    nc = tc.nc
    with ExitStack() as ctx:
        keep = ctx.enter_context(tc.tile_pool(name="keep", bufs=1))
        psum = ctx.enter_context(tc.psum_pool(name="psum", bufs=BANKS))

        def sbuf(name, width, dtype, after=None):
            return keep.tile([P, width], dtype, name=name, tag=after or name, align_bytes=64)

        def entries(list_tile, cols):
            return list_tile[:, cols.start // PER_COLUMN : cols.stop // PER_COLUMN]

        def load_scale_rows(queues, scale_tile, scales):
            for q in range(4):
                queues[q].dma_start(out=scale_tile[32 * q : 32 * q + 4, :].bitcast(I32), in_=scales[0, 4 * q : 4 * q + 4, :].bitcast(I32))

        def deal_words(engine, name, words, after=None):
            dealt = sbuf(name, 2 * H, U8, after)
            engine.tensor_copy(out=dealt[:].rearrange("p (t m b) -> p t m b", t=PACK, b=2), in_=words[:].rearrange("p (m t b) -> p t m b", t=PACK, b=2))
            return dealt

        def deal_scales(engine, name, scales, after=None):
            dealt = sbuf(name, H, U8, after)
            engine.tensor_copy(out=dealt[:].rearrange("p (t m) -> p t m", t=PACK), in_=scales[:].rearrange("p (m t) -> p t m", t=PACK))
            return dealt

        halves = [slice(h * BANK, (h + 1) * BANK) for h in range(S // BANK)]
        quarters = [slice(q * QUARTER, (q + 1) * QUARTER) for q in range(S // QUARTER)]
        pieces = [slice(c * PIECE, (c + 1) * PIECE) for c in range(U // PIECE)]

        offs_t = keep.tile([P, S // PER_COLUMN], U16, name="offs_t")
        env_t = keep.tile([P, S // PER_COLUMN], U16, name="env_t")
        stn_t = keep.tile([P, U // PER_COLUMN], U16, name="stn_t")
        xw = sbuf("xw", T, U32)
        xs = sbuf("xs", T, U8)
        w2w, w2s = sbuf("w2w", 2 * H, U8), sbuf("w2s", H, U8)
        nc.vector.memset(xs[:].bitcast(I32), 0)
        nc.gpsimd.memset(w2s[:].bitcast(I32), 0)

        nc.sync.dma_start(offs_t[:], offs)
        nc.sync.dma_start(out=w2w[:].bitcast(I32), in_=w2_words[0].bitcast(I32))
        nc.sync.dma_start(env_t[:], env)
        nc.sync.dma_start(out=xw[:].bitcast(I32), in_=x_words[0].rearrange("p n t -> p (n t)").bitcast(I32))
        load_scale_rows([nc.scalar] * 4, xs, x_scales)
        load_scale_rows([nc.scalar, nc.scalar, nc.gpsimd, nc.gpsimd], w2s, w2_scales)
        nc.sync.dma_start(stn_t[:], stn)

        picked_words, picked_scales = sbuf("picked_words", S, U32), sbuf("picked_scales", S, U8)

        def pick(cols):
            nc.vector.tensor_copy(out=picked_scales[:, cols], in_=xs[:].indirect(entries(offs_t, cols)))
            nc.vector.tensor_copy(out=picked_words[:, cols], in_=xw[:].indirect(entries(offs_t, cols)))

        w2_dealt_words = deal_words(nc.vector, "w2_dealt_words", w2w)
        pick(quarters[0])
        w2_dealt = (w2_dealt_words, deal_scales(nc.gpsimd, "w2_dealt_scales", w2s))
        for cols in quarters[1:]:
            pick(cols)

        w1w, w1s = sbuf("w1w", 2 * H, U8, after="w2w"), sbuf("w1s", H, U8, after="w2s")
        nc.sync.dma_start(out=w1w[:].bitcast(I32), in_=w1_words[0].bitcast(I32))
        nc.gpsimd.memset(w1s[:].bitcast(I32), 0)
        load_scale_rows([nc.sync] * 4, w1s, w1_scales)
        dz_t = keep.tile([P, PACK, S], F32, name="dz_t", tag="xw", align_bytes=64)
        nc.sync.dma_start(out=dz_t[:], in_=dz.rearrange("(p t) j -> p t j", t=PACK))

        def product(acc, dealt, t, cols):
            words, scales = dealt
            nc.tensor.matmul_mx(out=acc, lhsT=words[:, 2 * P * t : 2 * P * (t + 1)].bitcast(FP4X4), lhsT_scale=scales[:, P * t : P * (t + 1)],
                                rhs=picked_words[:, cols].bitcast(FP8X4), rhs_scale=picked_scales[:, cols], start=True, stop=True)

        moist = sbuf("moist", PACK * S, F32)
        moist_by_tile = moist[:].rearrange("p (t j) -> p t j", t=PACK)
        for cols in quarters:
            for t0 in range(0, PACK, 2):
                wv = psum.tile([P, 2, QUARTER], F32, name="bank")
                for e in range(2):
                    product(wv[:, e, :], w2_dealt, t0 + e, cols)
                nc.scalar.activation(out=moist_by_tile[:, t0 : t0 + 2, cols], in_=wv[:], func=ACT.Sigmoid, scale=-1.0)

        ratio = sbuf("ratio", S, F32)
        square = [sbuf(f"square{h}", BANK, F32) for h in range(len(halves))]
        for h, cols in enumerate(halves):
            nc.vector.tensor_tensor(out=square[h][:], in0=moist[:, cols], in1=moist[:, cols], op=ALU.mult)
        for h, cols in enumerate(halves):
            nc.vector.tensor_scalar_add(out=ratio[:, cols], in0=square[h][:], scalar1=1.0)
        for cols in halves:
            nc.vector.reciprocal(out=ratio[:, cols], in_=ratio[:, cols])
        w1_dealt = (deal_words(nc.gpsimd, "w1_dealt_words", w1w, after="square0"), deal_scales(nc.gpsimd, "w1_dealt_scales", w1s, after="square1"))
        w3w, w3s = sbuf("w3w", 2 * N, U8, after="w2w"), sbuf("w3s", N, U8, after="w2s")
        nc.gpsimd.memset(w3s[:].bitcast(I32), 0)
        nc.sync.dma_start(out=w3w[:].bitcast(I32), in_=w3_words[0].bitcast(I32))
        load_scale_rows([nc.sync] * 4, w3s, w3_scales)
        unit_t = sbuf("unit_t", PACK, F32, after="xs")
        nc.sync.dma_start(out=unit_t[:], in_=unit.rearrange("(p t) o -> p (t o)", t=PACK))
        nc.scalar.activation(out=moist[:, S:], in_=moist[:, S:], func=ACT.Ln, bias=LN_FLOOR)

        ident = sbuf("ident", P, F32)
        make_identity(nc, ident[:])

        hid = keep.tile([P, PACK, U], BF16, name="hid", align_bytes=64)
        temp = [sbuf(f"temp{t}", S, F32) for t in range(PACK)]
        gain = [sbuf(f"gain{t}", S, F32) for t in range(PACK)]
        theta = [sbuf(f"theta{t}", S, F32) for t in range(PACK)]
        partner = [sbuf(f"partner{t}", S, F32) for t in range(PACK)]
        sink = [sbuf(f"sink{t}", S, F32) for t in range(PACK)]

        first_tile_steps = [[halves[0]], quarters[2:]]
        for t in range(PACK):
            tile_moist = moist[:, t * S : (t + 1) * S]
            if t > 0:
                nc.scalar.activation(out=tile_moist, in_=tile_moist, func=ACT.Tanh, scale=-1.0)
            for h, cols in enumerate(halves):
                tp = psum.tile([P, BANK], F32, name="bank")
                product(tp[:], w1_dealt, t, cols)
                nc.scalar.activation(out=temp[t][:, cols], in_=tp[:], func=ACT.Tanh)
                if t == 0:
                    for step in first_tile_steps[h]:
                        nc.scalar.activation(out=gain[t][:, step], in_=ratio[:, step], func=ACT.Exp, scale=1.2, bias=-0.6)
            if t > 0:
                nc.scalar.activation(out=gain[t][:], in_=tile_moist, func=ACT.Exp, scale=0.6)

        def make_theta(t):
            for cols in first_tile_steps[0] + first_tile_steps[1] if t == 0 else [slice(0, S)]:
                nc.vector.scalar_tensor_tensor(out=theta[t][:, cols], in0=temp[t][:, cols], scalar=1.5, in1=gain[t][:, cols], op0=ALU.add, op1=ALU.mult)
            if t == 0:
                for cols in halves:
                    nc.vector.tensor_copy(out=partner[t][:, cols], in_=theta[t][:, cols])
            elif t < FUSED_TILES:
                nc.sync.dma_start(out=partner[t][:], in_=theta[t][:])
            else:
                for cols in halves:
                    nc.scalar.activation(out=partner[t][:, cols], in_=theta[t][:].indirect(entries(env_t, cols)), func=ACT.Copy)

        def compare(t):
            if t < FUSED_TILES:
                for cols in halves:
                    nc.vector.tensor_tensor(out=sink[t][:, cols], in0=theta[t][:].indirect(entries(env_t, cols)), in1=partner[t][:, cols], op=ALU.subtract)
            else:
                nc.vector.tensor_tensor(out=sink[t][:], in0=partner[t][:], in1=theta[t][:], op=ALU.subtract)

        def energy(t, after=None):
            lift = sbuf(f"lift{t}", S, F32, after)
            nc.vector.scalar_tensor_tensor(out=lift[:], in0=sink[t][:], scalar=0.0, in1=dz_t[:, t, :], op0=ALU.min, op1=ALU.mult)
            if t == LAST:
                levels = lift[:].rearrange("p (v a e) -> p v a e", a=2, e=2)
                sums = sbuf("sums", 2 * V, F32)
                pair_sums = sums[:].rearrange("p (v e) -> p v e", e=2)
                nc.vector.tensor_tensor(out=pair_sums, in0=levels[:, :, 0, :], in1=levels[:, :, 1, :], op=ALU.add)
                cape = sbuf("cape", V, F32)
                nc.vector.scalar_tensor_tensor(out=cape[:], in0=pair_sums[:, :, 0], scalar=-1.0, in1=pair_sums[:, :, 1], op0=ALU.mult, op1=ALU.subtract)
                return cape[:]
            turned = psum.tile([P, BANK], F32, name="bank")
            cape_turned = sbuf(f"cape_turned{t}", V, F32)
            cape = psum.tile([P, BANK], F32, name="bank")
            for b in range(V // P):
                for d in range(D):
                    nc.tensor.matmul(turned[:, b * P : (b + 1) * P], lift[:, b * D * P + d : (b + 1) * D * P : D], ident[:], is_transpose=True, start=(d == 0), stop=(d == D - 1))
            nc.scalar.activation(out=cape_turned[:], in_=turned[:, 0:V], func=ACT.Copy, scale=-1.0)
            for b in range(V // P):
                nc.tensor.transpose(cape[:, b * P : (b + 1) * P], cape_turned[:, b * P : (b + 1) * P], ident[:])
            return cape[:, 0:V]

        def inhibition(t, after=None):
            work = sbuf(f"work{t}", 3 * V, F32, after)
            cin, pair_max = work[:, 0:V], work[:, V : 3 * V].rearrange("p (v e) -> p v e", e=2)
            levels = sink[t][:].rearrange("p (v a e) -> p v a e", a=2, e=2)
            nc.vector.tensor_tensor(out=pair_max, in0=levels[:, :, 0, :], in1=levels[:, :, 1, :], op=ALU.max)
            nc.vector.scalar_tensor_tensor(out=cin, in0=pair_max[:, :, 0], scalar=0.0, in1=pair_max[:, :, 1], op0=ALU.max, op1=ALU.max)
            nc.scalar.activation(out=cin, in_=cin, func=ACT.Exp, scale=-1.0)
            return cin

        def stations(t, cape, damp, after=None):
            table = sbuf(f"table{t}", V, F32, after)
            nc.vector.scalar_tensor_tensor(out=table[:], in0=cape, scalar=unit_t[:, t : t + 1], in1=damp, op0=ALU.mult, op1=ALU.mult)
            for c, cols in enumerate(pieces):
                looked_up = table[:].indirect(entries(stn_t, cols))
                if t == LAST and c < VECTOR_PIECES:
                    nc.vector.tensor_copy(out=hid[:, t, cols], in_=looked_up)
                else:
                    nc.scalar.activation(out=hid[:, t, cols], in_=looked_up, func=ACT.Copy)

        make_theta(0)
        compare(0)
        make_theta(1)
        cape0 = energy(0, after="temp1")
        damp0 = inhibition(0, after="gain1")
        make_theta(2)
        compare(1)
        make_theta(3)
        cape1 = energy(1, after="temp3")
        damp1 = inhibition(1, after="gain3")
        compare(2)
        cape2 = energy(2)
        stations(0, cape0, damp0, after="partner2")
        compare(3)
        stations(1, cape1, damp1, after="partner3")
        damp2 = inhibition(2)
        cape3 = energy(3)
        damp3 = inhibition(3)
        stations(2, cape2, damp2)
        stations(3, cape3, damp3)

        for c, cols in enumerate(pieces):
            woven = keep.tile([P, PIECE, PACK], BF16, name=f"woven{c}", align_bytes=64)
            nc.vector.tensor_copy(out=woven[:].rearrange("p (g i) t -> p g t i", i=4), in_=hid[:, :, cols].rearrange("p t (g i) -> p g t i", i=4))
            hid_words, hid_scales = sbuf(f"hid_words{c}", PIECE, U32), sbuf(f"hid_scales{c}", PIECE, U8)
            nc.vector.quantize_mx(out=hid_words[:].bitcast(FP8X4), scales=hid_scales[:], in_=woven[:].rearrange("p r t -> p (r t)"))
            acc = psum.tile([P, BANK], F32, name="bank")
            nc.tensor.matmul_mx(out=acc[:, 0:PIECE], lhsT=w3w[:].bitcast(FP4X4), lhsT_scale=w3s[:], rhs=hid_words[:].bitcast(FP8X4), rhs_scale=hid_scales[:], start=True, stop=True)
            result = sbuf(f"result{c}", PIECE, F32)
            nc.scalar.copy(out=result[:], in_=acc[:, 0:PIECE])
            nc.sync.dma_start(out=out[:, cols], in_=result[:])
